import numpy as np, ml_dtypes
CORES = [211,219,227,235,243,251,83,91,99,107,115,123]
N = 12
import mx_ref
BF = ml_dtypes.bfloat16
def entries(a):
    return np.ascontiguousarray(a.T).reshape(-1)
def table(e):
    return np.ascontiguousarray(np.reshape(e, (-1, 16)).T).astype(np.int32)
def f(rng, *shape):
    return mx_ref.flush((rng.standard_normal(shape, dtype=np.float32) * np.exp2(rng.integers(-2, 3, shape[:-1] + (1,)))).astype(BF))
def wide(rng, *shape, cols=0):
    v = rng.standard_normal(shape, dtype=np.float32) * np.exp2(rng.integers(-12, 13, shape)).astype(np.float32)
    if cols: v *= np.repeat(np.exp2(rng.integers(-cols, cols + 1, shape[:-2] + (1, shape[-1] // 4))) * (rng.random(shape[:-2] + (1, shape[-1] // 4)) > 0.0625), 4, axis=-1).astype(np.float32)
    return mx_ref.flush(v.astype(BF))
T, CAPP, OC, UN = 192, 16, 84, 48
HOST = [0 if c < 128 else 1 for c in CORES]
def term(a, B):
    return np.stack([mx_ref.matmul(mx_ref.quantize(a[:, 512 * i:512 * i + 512]), B) for i in range(4)], axis=2).reshape(128, -1)
def padded(e, k):
    return table(np.concatenate([e, np.full(k - len(e), -1)]))
def lists(rng, fixed=False, blocks=False, plain=False, short=False):
    own = [[[] for d in range(N)] for r in range(N)]
    union = np.full((N, 2, UN), -1)
    for d in range(N):
        half = np.arange(OC) if blocks else rng.permutation(OC)
        ext = [rng.choice(half[(1 - g) * (OC // 2):(2 - g) * (OC // 2)], UN - OC // 2, replace=False) for g in range(2)]
        low = int(rng.integers(0, 2)) if short else -1
        for g in range(2):
            R = [r for r in range(N) if HOST[r] == g]
            mine = list(half[g * (OC // 2):(g + 1) * (OC // 2)]) + list(ext[g])
            p = rng.permutation(len(R)); named = [set() for _ in mine]
            for k in range(CAPP):
                if not fixed: p = rng.permutation(len(R))
                for i in range(len(R) // 2): named[k * (len(R) // 2) + i] = {R[p[2 * i]], R[p[2 * i + 1]]}
            if g == low:
                both = [j for j in range(UN) if j >= OC // 2 or mine[j] in ext[1 - g]]
                for j in both:
                    for r in list(named[j]):
                        to = [t for t in range(OC // 2) if t not in both and r not in named[t]]
                        named[j].remove(r); named[rng.choice(to)].add(r)
            elif not (plain or fixed or short):
                for j in range(OC // 2, UN):
                    for r in list(rng.permutation(list(named[j])))[:rng.integers(0, 3)]:
                        to = [t for t in range(OC // 2) if r not in named[t]]
                        named[j].remove(r); named[rng.choice(to)].add(r)
            at = rng.permutation(UN)
            for j, s in enumerate(named):
                if s: union[d, g, at[j]] = mine[j]
                for r in s: own[r][d].append((mine[j], at[j]))
    send, place, un = [], np.full((N, N, CAPP), -1), []
    for r in range(N):
        send.append(table(rng.permutation(T))); u = []
        for d in range(N):
            o = [own[r][d][i] for i in rng.permutation(CAPP)]
            place[d, r] = [v for v, _ in o]; u += [w for _, w in o]
        un.append(table(u))
    return {"send": np.stack(send), "place": np.stack([table(place[d].reshape(-1)) for d in range(N)]), "un": np.stack(un), "upl": np.stack([padded(union[d].reshape(-1), 96) for d in range(N)])}
def setup_inputs(rng):
    return {"a": f(rng, N, 128, 4 * 512), "b": f(rng, N, 128, 4 * T), **lists(rng)}
def setup_inputs_blocks(rng):
    return {**setup_inputs(rng), **lists(rng, blocks=True, plain=True)}
def setup_inputs_lossless(rng):
    d = setup_inputs(rng)
    a = np.zeros((N, 128, 4 * 128, 4), np.float32)
    for r in range(N):
        k = rng.integers(0, 512, size=4 * 128)
        a[r, k // 4, np.arange(4 * 128), k % 4] = 1.0
    size = 2.0 ** rng.integers(-4, 5, size=(N, OC)); b = rng.integers(-1, 2, size=(N, 128, T, 4)).astype(np.float64)
    for r in range(N):
        s = entries(d["send"][r]).reshape(N, CAPP)
        for o in range(N): b[r][:, s[o]] *= size[o][entries(d["place"][o]).reshape(N, CAPP)[r]][None, :, None]
    d["a"], d["b"] = a.reshape(N, 128, 4 * 512).astype(BF), b.reshape(N, 128, 4 * T).astype(np.float32).astype(BF)
    return d
def setup_inputs_pairs(rng):
    return {**setup_inputs(rng), **lists(rng, fixed=True)}
def setup_inputs_short(rng):
    return {**setup_inputs(rng), **lists(rng, short=True)}
def setup_inputs_spread(rng):
    d = setup_inputs(rng); d["b"] = wide(rng, N, 128, 4 * T); return d
def check_inputs(x):
    b = []
    seen = np.zeros((N, OC), int)
    for r in range(N):
        s, u = entries(x["send"][r]), entries(x["un"][r]).reshape(N, CAPP)
        if sorted(s.tolist()) != list(range(T)): b.append("send")
        if u.min() < 0 or u.max() >= UN: b.append("un")
        for o in range(N):
            p = entries(x["place"][o]).reshape(N, CAPP)[r]
            if p.min() < 0 or p.max() >= OC or len(set(p.tolist())) != CAPP: b.append("place")
            w = entries(x["upl"][o])[:2 * UN].reshape(2, UN)[HOST[r]]
            if (w[u[o]] != p).any(): b.append("upl")
            seen[o][p] += 1
    for o in range(N):
        for g in range(2):
            w = entries(x["upl"][o]); bad = w.min() < -1 or w.max() >= OC or (w[2 * UN:] != -1).any(); w = w[:2 * UN].reshape(2, UN)[g]; w = w[w >= 0]
            if len(set(w.tolist())) != len(w): b.append("upl twice")
    if seen.min() < 2: b.append("a column with fewer than two terms")
    return b
def reference(a, b, send, place, un, upl):
    Z = [term(a[r], mx_ref.quantize(b[r])).reshape(128, T, 4) for r in range(N)]
    y = np.zeros((N, 128, 4 * OC), np.float32)
    for o in range(N):
        parts = []
        for r in range(N):
            t = np.zeros((128, OC, 4), np.float32); t[:, entries(place[o]).reshape(N, CAPP)[r]] = Z[r][:, entries(send[r]).reshape(N, CAPP)[o]]
            parts.append(t.reshape(128, 4 * OC))
        y[o] = mx_ref.total(parts)
    return {"y": y}

import numpy as np
from concourse.bass import DstId, RemoteDMATransfer
from concourse.mybir import dt, AluOpType, ActivationFunctionType

UN, OC, H = 48, 84, 6
SITE = 2 * UN
SLOT = SITE + 128
WIN = 304
SEC = 52

F32, BF, I32, U16, X4, U8 = "float32", "bfloat16", "int32", "uint16", "float8_e4m3fn_x4", "uint8"
SCRATCH = {
    "lsend": ("sbuf", [128, 12], I32), "lun": ("sbuf", [128, 12], I32), "lupl": ("sbuf", [128, 6], I32),
    "base": ("sbuf", [128, 12], I32), "uo": ("sbuf", [128, 12], I32),
    "gofs": ("sbuf", [128, 12], U16), "sofs": ("sbuf", [128, 48], U16),
    "bt": ("sbuf", [128, 768], BF), "at": ("sbuf", [128, 2048], BF),
    "bc1": ("sbuf", [128, 256], BF), "bp": ("sbuf", [128, 768], BF), "bc2": ("sbuf", [128, 512], BF),
    "qa": ("sbuf", [128, 512], X4), "sa": ("sbuf", [128, 512], U8),
    "qb1": ("sbuf", [128, 192], X4), "sb1": ("sbuf", [128, 192], U8),
    "qb2": ("sbuf", [128, 128], X4), "sb2": ("sbuf", [128, 128], U8),
    "ones": ("sbuf", [128, 520], BF), "strip": ("sbuf", [128, 520], BF), "zt": ("sbuf", [128, 512], BF),
    "qe": ("sbuf", [128, 512], X4), "se": ("sbuf", [128, 512], U8),
    "zc": ("sbuf", [128, 512], BF),
    "h1": ("sbuf", [128, 768], BF), "h2": ("sbuf", [128, 768], BF), "h3": ("sbuf", [128, 896], BF),
    "qh1": ("sbuf", [128, 192], X4), "sh1": ("sbuf", [128, 192], U8),
    "qh2": ("sbuf", [128, 192], X4), "sh2": ("sbuf", [128, 192], U8),
    "qh3": ("sbuf", [128, 224], X4), "sh3": ("sbuf", [128, 224], U8),
    "land": ("sbuf", [128, 5 * SLOT], X4), "lsc": ("sbuf", [128, 5 * SLOT], U8),
    "mt": ("sbuf", [128, 512], BF), "qm": ("sbuf", [128, 128], X4), "sm": ("sbuf", [128, 128], U8),
    "rl": ("sbuf", [128, UN + 128], X4), "rs": ("sbuf", [128, UN + 128], U8),
    "lf": ("sbuf", [128, 4 * SEC], F32), "rf": ("sbuf", [128, 4 * SEC], F32),
    "yacc": ("sbuf", [128, 384], F32), "yo": ("sbuf", [128, 384], F32),
    "jc": ("sbuf", [128, 6], I32), "neg": ("sbuf", [128, 6], I32), "dump": ("sbuf", [128, 6], I32),
    "uplo": ("sbuf", [128, 6], I32), "uofs": ("sbuf", [128, 8], U16), "wv": ("sbuf", [128, UN], F32),
    "win": ("sbuf", [128, 2 * WIN], F32), "mi": ("sbuf", [128, 96], I32), "mj": ("sbuf", [128, 96], I32),
    "mask": ("sbuf", [128, 96], F32), "d0": ("sbuf", [128, 192], F32), "dm": ("sbuf", [128, 192], F32),
    "ds": ("sbuf", [128, 192], F32), "iofs": ("sbuf", [128, 12], U16),
    "px": ("psum", [128, 2048], F32), "py": ("psum", [128, 2048], F32),
}
SEMAPHORES = ["gs", "vs", "ss", "ts", "ldsend", "ldun", "ldupl", "ldb", "lda0", "lda1", "stored", "sent", "xarr"] + ["arr%d" % x for x in range(H)]


def rank_program(g, core, T, topo):
    rank = T.rank_of(core)
    if rank is None:
        return
    V, S, P, Y = g.vector, g.scalar, g.tensor, g.sync
    COPY = ActivationFunctionType.Copy
    half, me = rank // H, rank % H
    pair, odd = me // 2, me % 2
    peers = [T.cores[half * H + x] for x in range(H)]
    host = topo.host(core)

    count = {"gs": 0, "vs": 0, "ss": 0, "ts": 0}
    queues = {"g": g, "v": V, "s": S, "t": P, "y": Y}
    known = {q: {} for q in queues}

    def done(sem, ins):
        ins.then_inc(T.sem[sem], 1)
        count[sem] += 1
        return (sem, count[sem])

    def need(q, *tokens):
        best = {}
        for sem, n in tokens:
            best[sem] = max(n, best.get(sem, 0))
        for sem, n in best.items():
            if known[q].get(sem, 0) < n:
                queues[q].wait_ge(T.sem[sem], n)
                known[q][sem] = n

    S.dma_start(T.bt[:], T.b[:]).then_inc(T.sem.ldb, 16)
    for k in range(8):
        Y.dma_start(T.lsend[16 * k:16 * k + 16, :], T.send[:]).then_inc(T.sem.ldsend, 16)
    for k in range(8):
        S.dma_start(T.lun[16 * k:16 * k + 16, :], T.un[:]).then_inc(T.sem.ldun, 16)
    Y.dma_start(T.at[:, 0:1024], T.a[:, 0:1024]).then_inc(T.sem.lda0, 16)
    S.dma_start(T.at[:, 1024:2048], T.a[:, 1024:2048]).then_inc(T.sem.lda1, 16)
    for k in range(8):
        Y.dma_start(T.lupl[16 * k:16 * k + 16, :], T.upl[:]).then_inc(T.sem.ldupl, 16)
    LSEND, LUN, LUPL, LB, LA0, LA1 = ("ldsend", 128), ("ldun", 128), ("ldupl", 128), ("ldb", 16), ("lda0", 16), ("lda1", 16)

    k_base = done("gs", g.iota(T.base[:], [[UN, 2], [0, 3], [SITE, 2]], 0, 0))
    k_ones = done("vs", V.memset(T.ones[:], 1.0))
    need("g", k_ones)
    k_strip = done("gs", g.affine_select(T.strip[:], T.ones[:], [[1, 520]], AluOpType.is_equal, 0.0, -4, -4))
    k_jc = done("gs", g.iota(T.jc[:], [[16, 6]], 97, 1))
    k_wv = done("gs", g.iota(T.wv[:], [[1, UN]], 0, 0, allow_small_or_imprecise_dtypes=True))
    k_mi = done("gs", g.iota(T.mi[:], [[1, 96]], 128, -1))
    k_bp0 = done("vs", V.memset(T.bp[:], 0.0))
    k_h20 = done("vs", V.memset(T.h2[:], 0.0))
    k_h30 = done("vs", V.memset(T.h3[:], 0.0))
    need("v", k_strip)
    for t in range(4):
        k_e = done("vs", V.quantize_mx(T.qe[:, 128 * t:128 * t + 128], T.se[:, 128 * t:128 * t + 128], T.strip[:, 4 - t:516 - t]))

    groups = [(pair + 1) % 3, (pair + 2) % 3, pair]

    def picks(k):
        for h in range(2):
            c = H * h + 2 * groups[k]
            tok = done("vs", V.tensor_scalar(T.gofs[:, 4 * k + 2 * h:4 * k + 2 * h + 2], T.lsend[:, c:c + 2], 4, None, AluOpType.mult))
        return tok

    def places(k):
        for h in range(2):
            c = H * h + 2 * groups[k]
            tok = done("vs", V.tensor_scalar(T.sofs[:, 16 * k + 2 * h:16 * k + 2 * h + 2], T.uo[:, c:c + 2], 4, None, AluOpType.mult))
        need("v", tok)
        for t in (1, 2, 3):
            tok = done("vs", V.tensor_scalar(T.sofs[:, 16 * k + 4 * t:16 * k + 4 * t + 4], T.sofs[:, 16 * k:16 * k + 4], t, None, AluOpType.add))
        return tok

    need("v", LSEND)
    k_g1 = picks(0)
    need("v", LUN, k_base)
    k_uo = done("vs", V.tensor_tensor(T.uo[:], T.lun[:], T.base[:], AluOpType.add))
    picks(1)
    k_g23 = picks(2)
    need("v", k_uo)
    k_s1 = places(0)

    need("s", LB, k_g1)
    k_bc1 = [done("ss", S.activation(T.bc1[:, 64 * t:64 * t + 64], T.bt[:, t:768].indirect(T.gofs[:, 0:4]), COPY)) for t in range(4)]
    need("s", k_g23)
    for t in range(4):
        k_bc2 = done("ss", S.activation(T.bc2[:, t:512:4], T.bt[:, t:768].indirect(T.gofs[:, 4:12]), COPY))
    k_bp = k_bp0
    for u in range(2):
        need("v", k_bp, k_s1, k_bc1[2 * u + 1])
        k_bp = done("vs", V.tensor_copy(T.bp[:].indirect(T.sofs[:, 8 * u:8 * u + 8]), T.bc1[:, 128 * u:128 * u + 128]))
    need("v", k_bp)
    k_qb1 = done("vs", V.quantize_mx(T.qb1[:], T.sb1[:], T.bp[:]))
    k_qa = []
    for u, load in enumerate((LA0, LA1)):
        need("v", load)
        k_qa.append(done("vs", V.quantize_mx(T.qa[:, 256 * u:256 * u + 256], T.sa[:, 256 * u:256 * u + 256], T.at[:, 1024 * u:1024 * u + 1024])))
    need("v", k_bc2)
    k_qb2 = done("vs", V.quantize_mx(T.qb2[:], T.sb2[:], T.bc2[:]))

    k_px, k_py = [], []
    need("t", k_qb1)
    for i in range(4):
        need("t", k_qa[i // 2])
        k_px.append(done("ts", P.matmul_mx(T.px[:, 512 * i:512 * i + 192], T.qa[:, 128 * i:128 * i + 128], T.sa[:, 128 * i:128 * i + 128], T.qb1[:], T.sb1[:], True, True)))
    need("t", k_qb2)
    for i in range(4):
        k_py.append(done("ts", P.matmul_mx(T.py[:, 512 * i:512 * i + 128], T.qa[:, 128 * i:128 * i + 128], T.sa[:, 128 * i:128 * i + 128], T.qb2[:], T.sb2[:], True, True)))

    for i in (0, 2):
        need("v", k_px[i])
        k_c1v = done("vs", V.tensor_copy(T.h1[:, i:768:4], T.px[:, 512 * i:512 * i + 192]))
    for i in (1, 3):
        need("s", k_px[i])
        k_c1s = done("ss", S.activation(T.h1[:, i:768:4], T.px[:, 512 * i:512 * i + 192], COPY))
    need("v", k_c1v, k_c1s)
    k_h1 = done("vs", V.quantize_mx(T.qh1[:], T.sh1[:], T.h1[:]))
    k_zc = []
    for k in range(2):
        for t in range(4):
            need("s", k_py[t])
            tok = done("ss", S.activation(T.zc[:, 256 * k + 64 * t:256 * k + 64 * t + 64], T.py[:, 512 * t + 64 * k:512 * t + 64 * k + 64], COPY))
        k_zc.append(tok)
    k_s2 = places(1)
    k_s3 = places(2)
    need("v", k_s2, k_h20, k_zc[0])
    k_c2 = done("vs", V.tensor_copy(T.h2[:].indirect(T.sofs[:, 16:32]), T.zc[:, 0:256]))
    need("v", k_c2)
    k_h2 = done("vs", V.quantize_mx(T.qh2[:], T.sh2[:], T.h2[:]))
    need("v", k_s3, k_h30, k_zc[1])
    k_c3 = done("vs", V.tensor_copy(T.h3[:].indirect(T.sofs[:, 32:48]), T.zc[:, 256:512]))
    need("v", k_c3)
    k_h3 = done("vs", V.quantize_mx(T.qh3[:], T.sh3[:], T.h3[:]))

    def bits(engines):
        return sum(1 << e for e in engines)

    def slot(receiver, sender):
        return SLOT * (sender if sender < receiver else sender - 1)

    def transfer(x, engines, src, dst):
        rid, pid = topo.addr(peers[x], core)
        return RemoteDMATransfer(dst_ids=[DstId(rid=rid, pnc=pid)], dma_engine_mask=bits(engines), remote_sem=T.sem["arr%d" % me], srcs=[src], dsts=[dst])

    sent = 0
    for k, (tok, qh, sh) in enumerate(((k_h1, T.qh1, T.sh1), (k_h2, T.qh2, T.sh2))):
        need("g", tok)
        for plane in range(2):
            ts = []
            for e in range(2):
                x = 2 * groups[k] + e
                eng = topo.engines(core, peers[x])
                q = len(eng) // 4
                part = 2 * ((k + plane) % 2) + e
                at = slot(x, me)
                if plane:
                    src, dst = sh[:, SITE * e:SITE * e + SITE], T.lsc[:, at:at + SITE]
                else:
                    src, dst = qh[:, SITE * e:SITE * e + SITE].bitcast(dt.uint8), T.land[:, at:at + SITE].bitcast(dt.uint8)
                ts.append(transfer(x, eng[q * part:q * part + q], src, dst))
                sent += q
            g.remote_dma_fused(ts, local_sem=T.sem.sent)
    mate = me + 1 - 2 * odd
    eng = topo.engines(core, peers[mate])
    rid, pid = topo.addr(peers[mate], core)
    at, lo = slot(mate, me), SITE * (1 - odd)
    need("g", k_h3)
    g.remote_dma(T.land[:, at:at + SITE].bitcast(dt.uint8), T.qh3[:, lo:lo + SITE].bitcast(dt.uint8), T.sem["arr%d" % me], T.sem.sent, pid, rid, bits(eng))
    g.remote_dma(T.lsc[:, at:at + SITE], T.sh3[:, lo:lo + SITE], T.sem["arr%d" % me], T.sem.sent, pid, rid, bits(eng))
    sent += 2 * len(eng)

    k_zt = done("vs", V.memset(T.zt[:], 0.0))
    need("v", k_zt)
    for k in range(5):
        k_pad = done("vs", V.quantize_mx(T.land[:, SLOT * k + SITE:SLOT * (k + 1)], T.lsc[:, SLOT * k + SITE:SLOT * (k + 1)], T.zt[:]))
    k_rpad = done("vs", V.quantize_mx(T.rl[:, UN:UN + 128], T.rs[:, UN:UN + 128], T.zt[:]))

    def decode(t, out, codes, scales, c, start, stop):
        return done("ts", P.matmul_mx(out[:, 512 * t:512 * t + 128], T.qe[:, 128 * t:128 * t + 128], T.se[:, 128 * t:128 * t + 128], codes[:, c:c + 128], scales[:, c:c + 128], start, stop))

    need("t", k_h3, k_e, k_c1v, k_c1s)
    for t in range(4):
        decode(t, T.px, T.qh3, T.sh3, SITE * odd, True, False)
    need("t", k_pad)
    n8 = len(eng)
    first, second = (pair + 2) % 3, (pair + 1) % 3
    for x, n in ((2 * first, n8 // 2), (2 * first + 1, n8 // 2), (2 * second, n8 // 2), (2 * second + 1, n8 // 2), (mate, 2 * n8)):
        P.wait_ge(T.sem["arr%d" % x], n)
        k_acc = [decode(t, T.px, T.land, T.lsc, slot(me, x), False, x == mate) for t in range(4)]

    k_mt = done("vs", V.memset(T.mt[:, 4 * UN:512], 0.0))
    for t in range(4):
        done("vs", V.memset(T.lf[:, SEC * t + UN:SEC * t + SEC], 0.0))
        k_z0 = done("vs", V.memset(T.rf[:, SEC * t + UN:SEC * t + SEC], 0.0))
    k_win = done("vs", V.memset(T.win[:], float(UN)))
    k_d1 = done("vs", V.memset(T.d0[:], 1.0))
    need("v", LUPL, k_jc, k_wv, k_mi)
    k_ng = done("vs", V.tensor_scalar(T.neg[:], T.lupl[:], 0, None, AluOpType.is_lt))
    k_mj = done("vs", V.tensor_scalar(T.mj[:], T.mi[:], 15, None, AluOpType.bitwise_and))
    need("v", k_ng)
    k_dp = done("vs", V.tensor_tensor(T.dump[:], T.neg[:], T.jc[:], AluOpType.mult))
    k_d0 = done("vs", V.memset(T.d0[:, 0:192:16], 0.0))
    need("v", k_dp)
    k_uo2 = done("vs", V.tensor_tensor(T.uplo[:], T.lupl[:], T.dump[:], AluOpType.add))
    k_mk = done("vs", V.tensor_scalar(T.mask[:], T.mj[:], 0, None, AluOpType.is_equal))
    need("v", k_uo2)
    for q in range(2):
        k_uf = done("vs", V.tensor_copy(T.uofs[:, 4 * q:4 * q + 3], T.uplo[:, 3 * q:3 * q + 3]))
    need("v", k_uf, k_win)
    for q in range(2):
        k_sc = done("vs", V.tensor_copy(T.win[:, WIN * q:WIN * q + WIN].indirect(T.uofs[:, 4 * q:4 * q + 3]), T.wv[:]))
    need("v", k_sc, k_mk)
    for q in range(2):
        k_dm = done("vs", V.tensor_tensor(T.dm[:, 96 * q:96 * q + 96], T.win[:, WIN * q:WIN * q + 96], T.mask[:], AluOpType.mult))
    need("v", k_dm, k_d0)
    k_ds = done("vs", V.tensor_tensor_scan(T.ds[:], T.d0[:], T.dm[:], 0.0, AluOpType.mult, AluOpType.add))
    need("v", k_ds)
    k_io = done("vs", V.tensor_copy(T.iofs[:], T.ds[:, 15:192:16]))

    far = UN * (1 - half)
    for t in (0, 2):
        need("v", k_acc[t])
        k_mv = done("vs", V.tensor_copy(T.mt[:, t:4 * UN:4], T.px[:, 512 * t + far:512 * t + far + UN]))
    for t in (1, 3):
        need("s", k_acc[t])
        k_ms = done("ss", S.activation(T.mt[:, t:4 * UN:4], T.px[:, 512 * t + far:512 * t + far + UN], COPY))
    need("v", k_mv, k_ms, k_mt)
    k_qm = done("vs", V.quantize_mx(T.qm[:], T.sm[:], T.mt[:]))
    other = T.cores[(rank + H) % (2 * H)]
    rid, pid = topo.addr(other, core)
    eng = topo.engines(core, other)
    need("g", k_qm)
    g.remote_dma(T.rl[:, 0:UN].bitcast(dt.uint8), T.qm[:, 0:UN].bitcast(dt.uint8), T.sem.xarr, T.sem.sent, pid, rid, bits(eng))
    g.remote_dma(T.rs[:, 0:UN], T.sm[:, 0:UN], T.sem.xarr, T.sem.sent, pid, rid, bits(eng))
    sent += 2 * len(eng)

    near = UN * half
    need("s", k_mv, k_z0)
    for t in range(4):
        k_lf = done("ss", S.activation(T.lf[:, SEC * t:SEC * t + UN], T.px[:, 512 * t + near:512 * t + near + UN], COPY))
    need("s", k_lf, k_io)
    for t in range(4):
        k_ya = done("ss", S.activation(T.yacc[:, t:384:4], T.lf[:, SEC * t:SEC * t + UN + 1].indirect(T.iofs[:, 6 * host:6 * host + 6]), COPY))

    need("t", k_zc[1], k_rpad)
    P.wait_ge(T.sem.xarr, 2 * len(eng))
    k_r = [decode(t, T.py, T.rl, T.rs, 0, True, True) for t in range(4)]
    k_rf = []
    for t in range(4):
        need("s", k_r[t])
        k_rf.append(done("ss", S.activation(T.rf[:, SEC * t:SEC * t + UN], T.py[:, 512 * t:512 * t + UN], COPY)))
    need("v", k_ya)
    q = 6 * (1 - host)
    for t in range(4):
        need("v", k_rf[t])
        k_yo = done("vs", V.tensor_tensor(T.yo[:, t:384:4], T.rf[:, SEC * t:SEC * t + UN + 1].indirect(T.iofs[:, q:q + 6]), T.yacc[:, t:384:4], AluOpType.add))
    need("y", k_yo)
    Y.dma_start(T.y[:], T.yo[:, 0:4 * OC]).then_inc(T.sem.stored, 16)

    need("g", ("sent", sent), ("vs", count["vs"]), ("ss", count["ss"]), ("ts", count["ts"]), ("gs", count["gs"]), ("stored", 16))
